import numpy as np
import ml_dtypes


def mxq(x, axis, fmt="e4m3"):
    dtype, down = {"e4m3": (ml_dtypes.float8_e4m3fn, 7), "e5m2": (ml_dtypes.float8_e5m2, 14)}[fmt]
    v = np.moveaxis(np.asarray(x, np.float32).astype(ml_dtypes.bfloat16).astype(np.float64), axis, -1)
    blocks = v.reshape(v.shape[:-1] + (-1, 32))
    amax = np.abs(blocks).max(-1, keepdims=True)
    byte = np.maximum(np.where(amax > 0, np.frexp(amax)[1] - 1 + 127, 0) - down, 1)
    scale = np.exp2(byte - 127.0)
    codes = (blocks / scale).astype(np.float32).astype(dtype).astype(np.float64)
    return np.moveaxis((codes * scale).reshape(v.shape), -1, axis)


WIDE = False


def mx_kscale(k):
    if not WIDE:
        return np.ones(k)
    levels = np.array([10, -10, 5, -5, 0])
    if k % 512:
        return np.exp2(np.random.permutation(np.resize(levels, k // 32))).repeat(32)
    a = np.empty((k // 512, 16))
    for p in range(k // 512):
        a[p, :8] = np.random.permutation(np.resize(levels, 8))
        for g in range(8):
            far = levels[np.abs(levels - a[p, g]) >= 10]
            a[p, g + 8] = far[np.random.randint(len(far))]
    return np.exp2(a.ravel()).repeat(32)


def f64(x):
    return np.asarray(x).astype(np.float64)


def striped(idx):
    return np.tile(idx.reshape(-1, 16).T, (8, 1)).astype(np.uint16)


def unstriped(offs):
    return offs[:16].T.reshape(-1).astype(np.int64)


E2M1 = np.array([0.0, 0.5, 1.0, 1.5, 2.0, 3.0, 4.0, 6.0, -0.0, -0.5, -1.0, -1.5, -2.0, -3.0, -4.0, -6.0])


def pack_weight(w, fmt):
    k, n = w.shape
    w = f64(np.asarray(w, np.float32).astype(ml_dtypes.bfloat16)).reshape(k // 32, 32, n)
    amax = np.abs(w).max(1)
    if fmt == "e4m3":
        byte = np.frexp(amax)[1] - 1 + 127 - 7
    else:
        mant, ex = np.frexp(amax / 6.0)
        byte = np.where(mant > 0.5, ex, ex - 1) + 127
    byte = np.clip(np.where(amax > 0, byte, 1), 1, 254)
    scaled = (w * np.exp2(127.0 - byte)[:, None, :]).reshape(k, n).astype(np.float32)
    by_word = np.ascontiguousarray(scaled.reshape(k // 512, 128, 4, n).transpose(0, 1, 3, 2))
    if fmt == "e4m3":
        words = by_word.astype(ml_dtypes.float8_e4m3fn).view(np.uint8)
    else:
        c = by_word.astype(ml_dtypes.float4_e2m1fn).view(np.uint8) & 0xF
        words = (c[..., 0::2] | (c[..., 1::2] << 4)).reshape(k // 512, 128, 2 * n)
    return np.ascontiguousarray(words), np.ascontiguousarray(byte.astype(np.uint8).reshape(k // 512, 16, n))


def unpack_weight(words, scales, fmt):
    g, _, n = scales.shape
    words = np.ascontiguousarray(words).reshape(g, 128, n, -1)
    if fmt == "e4m3":
        vals = words.view(ml_dtypes.float8_e4m3fn).astype(np.float64)
    else:
        nib = np.empty((g, 128, n, 4), np.uint8)
        nib[..., 0::2] = words & 0xF
        nib[..., 1::2] = words >> 4
        vals = E2M1[nib]
    vals = vals * np.repeat(np.exp2(scales.astype(np.float64) - 127.0), 8, axis=1)[..., None]
    return vals.transpose(0, 1, 3, 2).reshape(g * 512, n)


def relu(v):
    return np.maximum(v, 0.0)


K, T, E, C, H, N = 512, 1536, 12, 128, 1024, 128


def by_expert(wq, xq):
    return np.concatenate([wq[e].T @ xq[:, e * C:(e + 1) * C] for e in range(E)], axis=1)


def setup_inputs():
    n = np.random.standard_normal
    s = mx_kscale(K)[:, None]
    u = mx_kscale(H)
    x = pack_weight(n((K, T)) * s, "e4m3")
    return {
        "x_words": x[0],
        "x_scales": x[1],
        "w1": (n((E, K, H)) / np.sqrt(K) / s[None] * u[None, None, :]).astype(np.float32),
        "w2": (n((E, H, N)) / np.sqrt(H) / u[None, :, None]).astype(np.float32),
        "gate": np.tile(np.random.uniform(0.2, 1.0, E * C), (N, 1)).astype(np.float32),
        "offs": striped(np.random.permutation(T)[:E * C]),
    }


def reference(x_words, x_scales, w1, w2, gate, offs):
    idx = unstriped(offs)
    xq = unpack_weight(x_words, x_scales, "e4m3")[:, idx]
    h = relu(by_expert(mxq(f64(w1), 1, "e4m3"), xq))
    y = by_expert(mxq(f64(w2), 1, "e4m3"), mxq(h, 0, "e4m3"))
    out = np.zeros((N, T))
    out[:, idx] = f64(gate) * y
    return out

@@ -1,0 +1,164 @@
+from contextlib import ExitStack
+
+import concourse.mybir as mybir
+
+K, T, E, C, H, N = 512, 1536, 12, 128, 1024, 128
+FLOPS = 2 * E * C * (K * H + H * N)
+
+F32 = mybir.dt.float32
+BF16 = mybir.dt.bfloat16
+I32 = mybir.dt.int32
+U32 = mybir.dt.uint32
+U16 = mybir.dt.uint16
+U8 = mybir.dt.uint8
+FP8X4 = mybir.dt.float8_e4m3fn_x4
+RELU = mybir.ActivationFunctionType.Relu
+MULT = mybir.AluOpType.mult
+
+P = 128
+PACK = 4
+PASS = P * PACK
+PASSES = H // PASS
+LANES = 16
+GATHER = 768
+SCATTER_ENDS = (256, 512, 768, 1024, 1280, 1536)
+
+
+def tile_moe_pkd_mlp_relu_kernel(tc, x_words, x_scales, w1, w2, gate, offs, out):
+    nc = tc.nc
+    with ExitStack() as ctx:
+        keep = ctx.enter_context(tc.tile_pool(name="keep", bufs=1))
+        w1_pool = ctx.enter_context(tc.tile_pool(name="w1_pool", bufs=5))
+        w2_pool = ctx.enter_context(tc.tile_pool(name="w2_pool", bufs=5))
+        work = ctx.enter_context(tc.tile_pool(name="work", bufs=3))
+        a_psum = ctx.enter_context(tc.psum_pool(name="a_psum", bufs=4))
+        y_psum = ctx.enter_context(tc.psum_pool(name="y_psum", bufs=2))
+
+        offsets = keep.tile([P, T // LANES], U16)
+        nc.sync.dma_start(offsets[:], offs)
+        token_words = keep.tile([P, T], I32, align_bytes=64)
+        nc.sync.dma_start(token_words[:], x_words[0].rearrange("p t r -> p (t r)").bitcast(I32))
+        token_scales = keep.tile([P, T], U8, align_bytes=64)
+        nc.gpsimd.memset(token_scales[:], 0)
+        for q in range(4):
+            nc.scalar.dma_start(token_scales[32 * q : 32 * q + 4, :].bitcast(I32), x_scales[0, 4 * q : 4 * q + 4, :].bitcast(I32))
+
+        gates = keep.tile([P, T], F32)
+        y_slots = keep.tile([P, T], F32)
+        result = keep.tile([P, T], F32)
+
+        w1_rows = {}
+        w2_rows = {}
+
+        def load_w1(e):
+            rows = w1[e].rearrange("(p j) i -> p j i", j=PACK)
+            if e < E - 1:
+                raw = w1_pool.tile([P, PACK, H], F32, name="w1_raw")
+                nc.sync.dma_start(raw[:], rows)
+                for a in range(PASSES):
+                    w1_rows[e, a] = raw[:, :, a * PASS : (a + 1) * PASS]
+            else:
+                raw = w1_pool.tile([P, PASSES, PACK, PASS], F32, name="w1_raw")
+                for a in range(PASSES):
+                    nc.sync.dma_start(raw[:, a], rows[:, :, a * PASS : (a + 1) * PASS])
+                    w1_rows[e, a] = raw[:, a]
+
+        def load_w2(e):
+            raw = w2_pool.tile([P, PASSES, PACK, N], F32, name="w2_raw")
+            nc.sync.dma_start(raw[:].rearrange("p a j n -> p a (j n)"), w2[e].rearrange("(a p j) n -> p a (j n)", a=PASSES, j=PACK))
+            w2_rows[e] = raw
+
+        def copy_on(engine, dst, src):
+            if engine == "scalar":
+                nc.scalar.copy(dst, src)
+            else:
+                nc.vector.tensor_copy(dst, src)
+
+        def quantize(values, name):
+            width = values.shape[1] // PACK
+            codes = work.tile([P, width], U32, name=name + "_codes", align_bytes=64)
+            scales = work.tile([P, width], U8, name=name + "_scales", align_bytes=64)
+            nc.vector.quantize_mx(codes[:].bitcast(FP8X4), scales[:], values)
+            return codes, scales
+
+        load_w1(0)
+        load_w1(1)
+        load_w2(0)
+        nc.sync.dma_start(gates[:], gate)
+        load_w1(2)
+        load_w2(1)
+
+        slot_words = []
+        slot_scales = []
+        for g in range(T // GATHER):
+            piece = offsets[:, g * GATHER // LANES : (g + 1) * GATHER // LANES]
+            words = keep.tile([P, GATHER], U32, name="slot_words%d" % g, align_bytes=64)
+            nc.vector.tensor_copy(words[:], token_words[:].bitcast(U32).indirect(piece))
+            scales = keep.tile([P, GATHER], U8, name="slot_scales%d" % g, align_bytes=64)
+            nc.vector.tensor_copy(scales[:], token_scales[:].indirect(piece))
+            slot_words.append(words)
+            slot_scales.append(scales)
+
+        def first_layer(e, a):
+            grouped = work.tile([P, PACK, P, PACK], BF16, name="w1_grouped%d" % a, align_bytes=64)
+            dst = grouped[:].rearrange("p t m j -> p m j t")
+            src = w1_rows[e, a].rearrange("p j (m t) -> p m j t", t=PACK)
+            if e < E - 1:
+                shares = [("scalar" if a == 0 else "vector", 0, P)]
+            else:
+                cut = 64 if a == 0 else 32
+                shares = [("scalar", 0, cut), ("vector", cut, P)]
+            for engine, m0, m1 in shares:
+                copy_on(engine, dst[:, m0:m1], src[:, m0:m1])
+            codes, scales = quantize(grouped[:].rearrange("p t m j -> p (t m j)"), "w1_%d" % a)
+            g, first = divmod(e * C, GATHER)
+            bank = a_psum.tile([P, PACK, C], F32, name="a_bank")
+            for t in range(PACK):
+                nc.tensor.matmul_mx(
+                    bank[:, t, :],
+                    lhsT=codes[:, t * P : (t + 1) * P].bitcast(FP8X4),
+                    lhsT_scale=scales[:, t * P : (t + 1) * P],
+                    rhs=slot_words[g][:, first : first + C].bitcast(FP8X4),
+                    rhs_scale=slot_scales[g][:, first : first + C],
+                    start=True,
+                    stop=True,
+                )
+            hidden = work.tile([P, C, PACK], BF16, name="hidden%d" % a, align_bytes=64)
+            nc.scalar.activation(hidden[:], bank[:].rearrange("p t s -> p s t"), RELU)
+            return quantize(hidden[:].rearrange("p s t -> p (s t)"), "h_%d" % a)
+
+        def second_layer(e, hidden_passes):
+            grouped = work.tile([P, PASSES, N, PACK], BF16, name="w2_grouped", align_bytes=64)
+            for a in range(PASSES):
+                copy_on(
+                    "scalar" if a == 0 else "vector",
+                    grouped[:, a].rearrange("p (c i) j -> p c j i", i=4),
+                    w2_rows[e][:, a].rearrange("p j (c i) -> p c j i", i=4),
+                )
+            codes, scales = quantize(grouped[:].rearrange("p a n j -> p (a n j)"), "w2")
+            bank = y_psum.tile([P, C], F32, name="y_bank")
+            for a, (h_codes, h_scales) in enumerate(hidden_passes):
+                nc.tensor.matmul_mx(
+                    bank[:],
+                    lhsT=codes[:, a * N : (a + 1) * N].bitcast(FP8X4),
+                    lhsT_scale=scales[:, a * N : (a + 1) * N],
+                    rhs=h_codes[:].bitcast(FP8X4),
+                    rhs_scale=h_scales[:],
+                    start=(a == 0),
+                    stop=(a == PASSES - 1),
+                )
+            nc.scalar.copy(y_slots[:, e * C : (e + 1) * C], bank[:])
+
+        done = 0
+        for e in range(E):
+            if e + 3 < E:
+                load_w1(e + 3)
+            if e + 2 < E:
+                load_w2(e + 2)
+            second_layer(e, [first_layer(e, a) for a in range(PASSES)])
+            for end in SCATTER_ENDS:
+                if done < end <= (e + 1) * C:
+                    piece = offsets[:, done // LANES : end // LANES]
+                    nc.vector.tensor_tensor(result[:].indirect(piece), y_slots[:, done:end], gates[:, done:end], MULT)
+                    done = end
+        nc.sync.dma_start(out, result[:])

@@ -20,16 +20,16 @@ PACK = 4
 PASS = P * PACK
 PASSES = H // PASS
 LANES = 16
-GATHER = 768
-SCATTER_ENDS = (256, 512, 768, 1024, 1280, 1536)
+GATHER = 384
+SCATTER_ENDS = (256, 512, 896, 1088, 1280, 1536)
 
 
 def tile_moe_pkd_mlp_relu_kernel(tc, x_words, x_scales, w1, w2, gate, offs, out):
     nc = tc.nc
     with ExitStack() as ctx:
         keep = ctx.enter_context(tc.tile_pool(name="keep", bufs=1))
-        w1_pool = ctx.enter_context(tc.tile_pool(name="w1_pool", bufs=5))
-        w2_pool = ctx.enter_context(tc.tile_pool(name="w2_pool", bufs=5))
+        w1_pool = ctx.enter_context(tc.tile_pool(name="w1_pool", bufs=7))
+        w2_pool = ctx.enter_context(tc.tile_pool(name="w2_pool", bufs=7))
         work = ctx.enter_context(tc.tile_pool(name="work", bufs=3))
         a_psum = ctx.enter_context(tc.psum_pool(name="a_psum", bufs=4))
         y_psum = ctx.enter_context(tc.psum_pool(name="y_psum", bufs=2))
@@ -38,10 +38,10 @@ def tile_moe_pkd_mlp_relu_kernel(tc, x_words, x_scales, w1, w2, gate, offs, out)
         nc.sync.dma_start(offsets[:], offs)
         token_words = keep.tile([P, T], I32, align_bytes=64)
         nc.sync.dma_start(token_words[:], x_words[0].rearrange("p t r -> p (t r)").bitcast(I32))
-        token_scales = keep.tile([P, T], U8, align_bytes=64)
-        nc.gpsimd.memset(token_scales[:], 0)
+        token_scales = keep.tile([P, T // 4], I32, align_bytes=64)
+        nc.vector.memset(token_scales[:], 0)
         for q in range(4):
-            nc.scalar.dma_start(token_scales[32 * q : 32 * q + 4, :].bitcast(I32), x_scales[0, 4 * q : 4 * q + 4, :].bitcast(I32))
+            nc.sync.dma_start(token_scales[32 * q : 32 * q + 4, :], x_scales[0, 4 * q : 4 * q + 4, :].bitcast(I32))
 
         gates = keep.tile([P, T], F32)
         y_slots = keep.tile([P, T], F32)
@@ -52,7 +52,7 @@ def tile_moe_pkd_mlp_relu_kernel(tc, x_words, x_scales, w1, w2, gate, offs, out)
 
         def load_w1(e):
             rows = w1[e].rearrange("(p j) i -> p j i", j=PACK)
-            if e < E - 1:
+            if e < 11:
                 raw = w1_pool.tile([P, PACK, H], F32, name="w1_raw")
                 nc.sync.dma_start(raw[:], rows)
                 for a in range(PASSES):
@@ -63,10 +63,19 @@ def tile_moe_pkd_mlp_relu_kernel(tc, x_words, x_scales, w1, w2, gate, offs, out)
                     nc.sync.dma_start(raw[:, a], rows[:, :, a * PASS : (a + 1) * PASS])
                     w1_rows[e, a] = raw[:, a]
 
-        def load_w2(e):
-            raw = w2_pool.tile([P, PASSES, PACK, N], F32, name="w2_raw")
-            nc.sync.dma_start(raw[:].rearrange("p a j n -> p a (j n)"), w2[e].rearrange("(a p j) n -> p a (j n)", a=PASSES, j=PACK))
+        def load_w2(e, raw):
+            nc.sync.dma_start(raw.rearrange("p a j n -> p a (j n)"), w2[e].rearrange("(a p j) n -> p a (j n)", a=PASSES, j=PACK))
             w2_rows[e] = raw
+
+        def load(e):
+            load_w1(e)
+            if e < E - 2:
+                raw = w2_pool.tile([P, PASSES, PACK, N], F32, name="w2_raw")
+                load_w2(e, raw[:])
+            elif e == E - 1:
+                raw = w1_pool.tile([P, 2, PASSES, PACK, N], F32, name="w1_raw")
+                load_w2(E - 2, raw[:, 0])
+                load_w2(E - 1, raw[:, 1])
 
         def copy_on(engine, dst, src):
             if engine == "scalar":
@@ -81,84 +90,106 @@ def tile_moe_pkd_mlp_relu_kernel(tc, x_words, x_scales, w1, w2, gate, offs, out)
             nc.vector.quantize_mx(codes[:].bitcast(FP8X4), scales[:], values)
             return codes, scales
 
-        load_w1(0)
-        load_w1(1)
-        load_w2(0)
+        load(0)
         nc.sync.dma_start(gates[:], gate)
-        load_w1(2)
-        load_w2(1)
+        load(1)
+        load(2)
 
-        slot_words = []
-        slot_scales = []
-        for g in range(T // GATHER):
+        slot_words = {}
+        slot_scales = {}
+
+        def gather(g):
             piece = offsets[:, g * GATHER // LANES : (g + 1) * GATHER // LANES]
-            words = keep.tile([P, GATHER], U32, name="slot_words%d" % g, align_bytes=64)
-            nc.vector.tensor_copy(words[:], token_words[:].bitcast(U32).indirect(piece))
-            scales = keep.tile([P, GATHER], U8, name="slot_scales%d" % g, align_bytes=64)
-            nc.vector.tensor_copy(scales[:], token_scales[:].indirect(piece))
-            slot_words.append(words)
-            slot_scales.append(scales)
+            slot_words[g] = keep.tile([P, GATHER], U32, name="slot_words%d" % g, align_bytes=64)
+            nc.vector.tensor_copy(slot_words[g][:], token_words[:].bitcast(U32).indirect(piece))
+            slot_scales[g] = keep.tile([P, GATHER], U8, name="slot_scales%d" % g, align_bytes=64)
+            nc.vector.tensor_copy(slot_scales[g][:], token_scales[:].bitcast(U8).indirect(piece))
 
-        def first_layer(e, a):
-            grouped = work.tile([P, PACK, P, PACK], BF16, name="w1_grouped%d" % a, align_bytes=64)
-            dst = grouped[:].rearrange("p t m j -> p m j t")
+        def quantize_blocks(values, name):
+            codes, scales = quantize(values.rearrange("p b c j -> p (b c j)"), name)
+            return [(codes[:, b * P : (b + 1) * P], scales[:, b * P : (b + 1) * P]) for b in range(values.shape[1])]
+
+        def cast_w1(e, a, cut, blocks):
+            dst = blocks.rearrange("p t m j -> p m j t")
             src = w1_rows[e, a].rearrange("p j (m t) -> p m j t", t=PACK)
-            if e < E - 1:
-                shares = [("scalar" if a == 0 else "vector", 0, P)]
-            else:
-                cut = 64 if a == 0 else 32
-                shares = [("scalar", 0, cut), ("vector", cut, P)]
-            for engine, m0, m1 in shares:
-                copy_on(engine, dst[:, m0:m1], src[:, m0:m1])
-            codes, scales = quantize(grouped[:].rearrange("p t m j -> p (t m j)"), "w1_%d" % a)
-            g, first = divmod(e * C, GATHER)
-            bank = a_psum.tile([P, PACK, C], F32, name="a_bank")
-            for t in range(PACK):
-                nc.tensor.matmul_mx(
-                    bank[:, t, :],
-                    lhsT=codes[:, t * P : (t + 1) * P].bitcast(FP8X4),
-                    lhsT_scale=scales[:, t * P : (t + 1) * P],
-                    rhs=slot_words[g][:, first : first + C].bitcast(FP8X4),
-                    rhs_scale=slot_scales[g][:, first : first + C],
-                    start=True,
-                    stop=True,
-                )
-            hidden = work.tile([P, C, PACK], BF16, name="hidden%d" % a, align_bytes=64)
-            nc.scalar.activation(hidden[:], bank[:].rearrange("p t s -> p s t"), RELU)
-            return quantize(hidden[:].rearrange("p s t -> p (s t)"), "h_%d" % a)
+            if cut > 0:
+                nc.scalar.copy(dst[:, :cut], src[:, :cut])
+            if cut < P:
+                nc.vector.tensor_copy(dst[:, cut:], src[:, cut:])
 
-        def second_layer(e, hidden_passes):
-            grouped = work.tile([P, PASSES, N, PACK], BF16, name="w2_grouped", align_bytes=64)
+        def cast_w2(e, blocks, engines):
             for a in range(PASSES):
                 copy_on(
-                    "scalar" if a == 0 else "vector",
-                    grouped[:, a].rearrange("p (c i) j -> p c j i", i=4),
+                    engines[a],
+                    blocks[:, a].rearrange("p (c i) j -> p c j i", i=4),
                     w2_rows[e][:, a].rearrange("p j (c i) -> p c j i", i=4),
                 )
-            codes, scales = quantize(grouped[:].rearrange("p a n j -> p (a n j)"), "w2")
-            bank = y_psum.tile([P, C], F32, name="y_bank")
-            for a, (h_codes, h_scales) in enumerate(hidden_passes):
-                nc.tensor.matmul_mx(
-                    bank[:],
-                    lhsT=codes[:, a * N : (a + 1) * N].bitcast(FP8X4),
-                    lhsT_scale=scales[:, a * N : (a + 1) * N],
-                    rhs=h_codes[:].bitcast(FP8X4),
-                    rhs_scale=h_scales[:],
-                    start=(a == 0),
-                    stop=(a == PASSES - 1),
-                )
-            nc.scalar.copy(y_slots[:, e * C : (e + 1) * C], bank[:])
 
-        done = 0
-        for e in range(E):
+        def matmul(dst, stationary, moving, start, stop):
+            nc.tensor.matmul_mx(
+                dst,
+                lhsT=stationary[0].bitcast(FP8X4),
+                lhsT_scale=stationary[1],
+                rhs=moving[0].bitcast(FP8X4),
+                rhs_scale=moving[1],
+                start=start,
+                stop=stop,
+            )
+
+        def first_layer(e, w1_blocks, hidden, engine):
+            g, first = divmod(e * C, GATHER)
+            tokens = (slot_words[g][:, first : first + C], slot_scales[g][:, first : first + C])
+            bank = a_psum.tile([P, PACK, C], F32, name="a_bank")
+            for t in range(PACK):
+                matmul(bank[:, t, :], w1_blocks[t], tokens, True, True)
+            if engine == "scalar":
+                nc.scalar.activation(hidden, bank[:].rearrange("p t s -> p s t"), RELU)
+            else:
+                nc.vector.tensor_scalar_max(hidden, bank[:].rearrange("p t s -> p s t"), 0.0)
+
+        def second_layer(e, h_blocks, w2_blocks):
+            bank = y_psum.tile([P, C], F32, name="y_bank")
+            for a in range(PASSES):
+                matmul(bank[:], w2_blocks[a], h_blocks[a], a == 0, a == PASSES - 1)
+            slots = slice(e * C, (e + 1) * C)
+            nc.vector.tensor_tensor(y_slots[:, slots], bank[:], gates[:, slots], MULT)
+            starts = (0,) + SCATTER_ENDS
+            for start, end in zip(starts, SCATTER_ENDS):
+                if e * C < end <= (e + 1) * C:
+                    piece = offsets[:, start // LANES : end // LANES]
+                    nc.vector.tensor_copy(result[:].indirect(piece), y_slots[:, start:end])
+
+        batch = work.tile([P, 2 * PACK, P, PACK], BF16, name="batch", align_bytes=64)
+        for e in range(E - 1):
             if e + 3 < E:
-                load_w1(e + 3)
-            if e + 2 < E:
-                load_w2(e + 2)
-            second_layer(e, [first_layer(e, a) for a in range(PASSES)])
-            for end in SCATTER_ENDS:
-                if done < end <= (e + 1) * C:
-                    piece = offsets[:, done // LANES : end // LANES]
-                    nc.vector.tensor_tensor(result[:].indirect(piece), y_slots[:, done:end], gates[:, done:end], MULT)
-                    done = end
+                load(e + 3)
+            if e * C % GATHER == 0:
+                gather(e * C // GATHER)
+            upper = work.tile([P, PACK, P, PACK], BF16, name="upper", align_bytes=64)
+            cast_w1(e, 0, 0 if e == E - 2 else 0, batch[:, :PACK])
+            cast_w1(e, 1, 128 if e == E - 2 else 128, upper[:])
+            if e > 0:
+                blocks = quantize_blocks(batch[:], "batch")
+                second_layer(e - 1, blocks[PACK : PACK + PASSES], blocks[PACK + PASSES :])
+            else:
+                blocks = quantize_blocks(batch[:, :PACK], "batch")
+            following = work.tile([P, 2 * PACK, P, PACK], BF16, name="batch", align_bytes=64)
+            first_layer(e, blocks[:PACK], following[:, PACK], "scalar")
+            first_layer(e, quantize_blocks(upper[:], "upper"), following[:, PACK + 1], "scalar")
+            if e < E - 2:
+                cast_w2(e, following[:, PACK + PASSES :], ["scalar", "scalar"])
+            batch = following
+        e = E - 1
+        upper = work.tile([P, PACK, P, PACK], BF16, name="upper", align_bytes=64)
+        following = work.tile([P, 2 * PACK, P, PACK], BF16, name="batch", align_bytes=64)
+        cast_w1(e, 0, 128, batch[:, :PACK])
+        first_layer(e, quantize_blocks(batch[:, :PACK], "batch"), following[:, PACK], "scalar")
+        cast_w2(e - 1, batch[:, PACK + PASSES :], ["scalar","scalar"])
+        blocks = quantize_blocks(batch[:, PACK:], "batch")
+        second_layer(e - 1, blocks[:PASSES], blocks[PASSES:])
+        cast_w1(e, 1, 32, upper[:])
+        first_layer(e, quantize_blocks(upper[:], "upper"), following[:, PACK + 1], "scalar")
+        cast_w2(e, following[:, PACK + PASSES :], ["scalar","vector"])
+        h_blocks = [quantize_blocks(following[:, PACK + a : PACK + a + 1], "upper")[0] for a in range(PASSES)]
+        second_layer(e, h_blocks, quantize_blocks(following[:, PACK + PASSES :], "batch"))
         nc.sync.dma_start(out, result[:])

@@ -21,15 +21,29 @@ PASS = P * PACK
 PASSES = H // PASS
 LANES = 16
 GATHER = 384
-SCATTER_ENDS = (256, 512, 896, 1088, 1280, 1536)
+SCATTER_ENDS = (256, 512, 768, 960, 1152, 1344, 1536)
+
+W1_LOADS = [(0, 256), (0, 256), (0, 256), (0, 256), (0, 256), (0, 256), (0, 256), (0, 256), (0, 256), (0, 256), (0, 256), (0, 64, 160, 256)]
+W1_CASTS = [((0, 128, "vector"), (128, 224, "scalar"), (224, 256, "vector"),),
+    ((0, 128, "vector"), (128, 224, "scalar"), (224, 256, "vector"),),
+    ((0, 128, "vector"), (128, 224, "scalar"), (224, 256, "vector"),),
+    ((0, 128, "vector"), (128, 224, "scalar"), (224, 256, "vector"),),
+    ((0, 128, "vector"), (128, 224, "scalar"), (224, 256, "vector"),),
+    ((0, 128, "vector"), (128, 224, "scalar"), (224, 256, "vector"),),
+    ((0, 128, "vector"), (128, 224, "scalar"), (224, 256, "vector"),),
+    ((0, 128, "vector"), (128, 224, "scalar"), (224, 256, "vector"),),
+    ((0, 128, "vector"), (128, 224, "scalar"), (224, 256, "vector"),),
+    ((0, 128, "vector"), (128, 224, "scalar"), (224, 256, "vector"),),
+    ((0, 128, "vector"), (128, 224, "scalar"), (224, 256, "vector"),),
+    ((0, 64, "scalar"), (64, 128, "vector"), (128, 160, "scalar"), (160, 256, "vector"),)]
 
 
 def tile_moe_pkd_mlp_relu_kernel(tc, x_words, x_scales, w1, w2, gate, offs, out):
     nc = tc.nc
     with ExitStack() as ctx:
         keep = ctx.enter_context(tc.tile_pool(name="keep", bufs=1))
-        w1_pool = ctx.enter_context(tc.tile_pool(name="w1_pool", bufs=7))
-        w2_pool = ctx.enter_context(tc.tile_pool(name="w2_pool", bufs=7))
+        w1_pool = ctx.enter_context(tc.tile_pool(name="w1_pool", bufs=6))
+        w2_pool = ctx.enter_context(tc.tile_pool(name="w2_pool", bufs=6))
         work = ctx.enter_context(tc.tile_pool(name="work", bufs=3))
         a_psum = ctx.enter_context(tc.psum_pool(name="a_psum", bufs=4))
         y_psum = ctx.enter_context(tc.psum_pool(name="y_psum", bufs=2))
@@ -52,16 +66,12 @@ def tile_moe_pkd_mlp_relu_kernel(tc, x_words, x_scales, w1, w2, gate, offs, out)
 
         def load_w1(e):
             rows = w1[e].rearrange("(p j) i -> p j i", j=PACK)
-            if e < 11:
-                raw = w1_pool.tile([P, PACK, H], F32, name="w1_raw")
-                nc.sync.dma_start(raw[:], rows)
-                for a in range(PASSES):
-                    w1_rows[e, a] = raw[:, :, a * PASS : (a + 1) * PASS]
-            else:
-                raw = w1_pool.tile([P, PASSES, PACK, PASS], F32, name="w1_raw")
-                for a in range(PASSES):
-                    nc.sync.dma_start(raw[:, a], rows[:, :, a * PASS : (a + 1) * PASS])
-                    w1_rows[e, a] = raw[:, a]
+            raw = w1_pool.tile([P, PACK * H], F32, name="w1_raw")
+            w1_rows[e] = []
+            for lo, hi in zip(W1_LOADS[e], W1_LOADS[e][1:]):
+                piece = raw[:, PACK * PACK * lo : PACK * PACK * hi].rearrange("p (j i) -> p j i", j=PACK)
+                nc.sync.dma_start(piece, rows[:, :, PACK * lo : PACK * hi])
+                w1_rows[e].append((lo, hi, piece.rearrange("p j (m t) -> p m j t", t=PACK)))
 
         def load_w2(e, raw):
             nc.sync.dma_start(raw.rearrange("p a j n -> p a (j n)"), w2[e].rearrange("(a p j) n -> p a (j n)", a=PASSES, j=PACK))
@@ -109,13 +119,12 @@ def tile_moe_pkd_mlp_relu_kernel(tc, x_words, x_scales, w1, w2, gate, offs, out)
             codes, scales = quantize(values.rearrange("p b c j -> p (b c j)"), name)
             return [(codes[:, b * P : (b + 1) * P], scales[:, b * P : (b + 1) * P]) for b in range(values.shape[1])]
 
-        def cast_w1(e, a, cut, blocks):
+        def cast_w1(e, a, blocks):
             dst = blocks.rearrange("p t m j -> p m j t")
-            src = w1_rows[e, a].rearrange("p j (m t) -> p m j t", t=PACK)
-            if cut > 0:
-                nc.scalar.copy(dst[:, :cut], src[:, :cut])
-            if cut < P:
-                nc.vector.tensor_copy(dst[:, cut:], src[:, cut:])
+            for lo, hi, engine in W1_CASTS[e]:
+                if lo // P == a:
+                    first, src = [(start, piece) for start, stop, piece in w1_rows[e] if start <= lo and hi <= stop][0]
+                    copy_on(engine, dst[:, lo - a * P : hi - a * P], src[:, lo - first : hi - first])
 
         def cast_w2(e, blocks, engines):
             for a in range(PASSES):
@@ -166,8 +175,8 @@ def tile_moe_pkd_mlp_relu_kernel(tc, x_words, x_scales, w1, w2, gate, offs, out)
             if e * C % GATHER == 0:
                 gather(e * C // GATHER)
             upper = work.tile([P, PACK, P, PACK], BF16, name="upper", align_bytes=64)
-            cast_w1(e, 0, 0 if e == E - 2 else 0, batch[:, :PACK])
-            cast_w1(e, 1, 128 if e == E - 2 else 128, upper[:])
+            cast_w1(e, 0, batch[:, :PACK])
+            cast_w1(e, 1, upper[:])
             if e > 0:
                 blocks = quantize_blocks(batch[:], "batch")
                 second_layer(e - 1, blocks[PACK : PACK + PASSES], blocks[PACK + PASSES :])
@@ -182,14 +191,14 @@ def tile_moe_pkd_mlp_relu_kernel(tc, x_words, x_scales, w1, w2, gate, offs, out)
         e = E - 1
         upper = work.tile([P, PACK, P, PACK], BF16, name="upper", align_bytes=64)
         following = work.tile([P, 2 * PACK, P, PACK], BF16, name="batch", align_bytes=64)
-        cast_w1(e, 0, 128, batch[:, :PACK])
+        cast_w1(e, 0, batch[:, :PACK])
         first_layer(e, quantize_blocks(batch[:, :PACK], "batch"), following[:, PACK], "scalar")
         cast_w2(e - 1, batch[:, PACK + PASSES :], ["scalar","scalar"])
         blocks = quantize_blocks(batch[:, PACK:], "batch")
         second_layer(e - 1, blocks[:PASSES], blocks[PASSES:])
-        cast_w1(e, 1, 32, upper[:])
+        cast_w1(e, 1, upper[:])
         first_layer(e, quantize_blocks(upper[:], "upper"), following[:, PACK + 1], "scalar")
         cast_w2(e, following[:, PACK + PASSES :], ["scalar","vector"])
-        h_blocks = [quantize_blocks(following[:, PACK + a : PACK + a + 1], "upper")[0] for a in range(PASSES)]
-        second_layer(e, h_blocks, quantize_blocks(following[:, PACK + PASSES :], "batch"))
+        w2_blocks = quantize_blocks(following[:, PACK + PASSES :], "batch")
+        second_layer(e, quantize_blocks(following[:, PACK : PACK + PASSES], "upper"), w2_blocks)
         nc.sync.dma_start(out, result[:])

@@ -19,120 +19,131 @@ P = 128
 PACK = 4
 PASS = P * PACK
 PASSES = H // PASS
-LANES = 16
-GATHER = 384
+QUADRANT = 32
+OFFSETS_PER_COLUMN = 16
+LINE = 4
+LAST = E - 1
+
+GATHER = 3 * C
 SCATTER_ENDS = (256, 512, 768, 960, 1152, 1344, 1536)
 
-W1_LOADS = [(0, 256), (0, 256), (0, 256), (0, 256), (0, 256), (0, 256), (0, 256), (0, 256), (0, 256), (0, 256), (0, 256), (0, 64, 160, 256)]
-W1_CASTS = [((0, 128, "vector"), (128, 224, "scalar"), (224, 256, "vector"),),
-    ((0, 128, "vector"), (128, 224, "scalar"), (224, 256, "vector"),),
-    ((0, 128, "vector"), (128, 224, "scalar"), (224, 256, "vector"),),
-    ((0, 128, "vector"), (128, 224, "scalar"), (224, 256, "vector"),),
-    ((0, 128, "vector"), (128, 224, "scalar"), (224, 256, "vector"),),
-    ((0, 128, "vector"), (128, 224, "scalar"), (224, 256, "vector"),),
-    ((0, 128, "vector"), (128, 224, "scalar"), (224, 256, "vector"),),
-    ((0, 128, "vector"), (128, 224, "scalar"), (224, 256, "vector"),),
-    ((0, 128, "vector"), (128, 224, "scalar"), (224, 256, "vector"),),
-    ((0, 128, "vector"), (128, 224, "scalar"), (224, 256, "vector"),),
-    ((0, 128, "vector"), (128, 224, "scalar"), (224, 256, "vector"),),
-    ((0, 64, "scalar"), (64, 128, "vector"), (128, 160, "scalar"), (160, 256, "vector"),)]
+W1_LOAD = (0, 256)
+W1_COPIES = ((0, 128, "vector"), (128, 224, "scalar"), (224, 256, "vector"))
+LAST_W1_LOAD = (0, 64, 160, 256)
+LAST_W1_COPIES = ((0, 64, "scalar"), (64, 128, "vector"), (128, 160, "scalar"), (160, 256, "vector"))
+
+LOAD_AHEAD = 3
+STREAM_BUFS = 6
+WORK_BUFS = 3
+A_BANKS = 4
+Y_BANKS = 2
+
+W1_PANELS = slice(0, PACK)
+H_PANELS = slice(PACK, PACK + PASSES)
+W2_PANELS = slice(PACK + PASSES, 2 * PACK)
+SECOND_LAYER_PANELS = slice(PACK, 2 * PACK)
 
 
 def tile_moe_pkd_mlp_relu_kernel(tc, x_words, x_scales, w1, w2, gate, offs, out):
     nc = tc.nc
+    copy = {"scalar": nc.scalar.copy, "vector": nc.vector.tensor_copy}
     with ExitStack() as ctx:
         keep = ctx.enter_context(tc.tile_pool(name="keep", bufs=1))
-        w1_pool = ctx.enter_context(tc.tile_pool(name="w1_pool", bufs=6))
-        w2_pool = ctx.enter_context(tc.tile_pool(name="w2_pool", bufs=6))
-        work = ctx.enter_context(tc.tile_pool(name="work", bufs=3))
-        a_psum = ctx.enter_context(tc.psum_pool(name="a_psum", bufs=4))
-        y_psum = ctx.enter_context(tc.psum_pool(name="y_psum", bufs=2))
+        w1_pool = ctx.enter_context(tc.tile_pool(name="w1_pool", bufs=STREAM_BUFS))
+        w2_pool = ctx.enter_context(tc.tile_pool(name="w2_pool", bufs=4))
+        work = ctx.enter_context(tc.tile_pool(name="work", bufs=WORK_BUFS))
+        a_psum = ctx.enter_context(tc.psum_pool(name="a_psum", bufs=A_BANKS))
+        y_psum = ctx.enter_context(tc.psum_pool(name="y_psum", bufs=Y_BANKS))
 
-        offsets = keep.tile([P, T // LANES], U16)
+        offsets = keep.tile([P, T // OFFSETS_PER_COLUMN], U16)
         nc.sync.dma_start(offsets[:], offs)
         token_words = keep.tile([P, T], I32, align_bytes=64)
         nc.sync.dma_start(token_words[:], x_words[0].rearrange("p t r -> p (t r)").bitcast(I32))
         token_scales = keep.tile([P, T // 4], I32, align_bytes=64)
         nc.vector.memset(token_scales[:], 0)
-        for q in range(4):
-            nc.sync.dma_start(token_scales[32 * q : 32 * q + 4, :], x_scales[0, 4 * q : 4 * q + 4, :].bitcast(I32))
+        for quadrant in range(P // QUADRANT):
+            nc.sync.dma_start(
+                token_scales[QUADRANT * quadrant : QUADRANT * quadrant + 4, :],
+                x_scales[0, 4 * quadrant : 4 * quadrant + 4, :].bitcast(I32),
+            )
 
         gates = keep.tile([P, T], F32)
         y_slots = keep.tile([P, T], F32)
         result = keep.tile([P, T], F32)
 
-        w1_rows = {}
+        w1_pieces = {}
         w2_rows = {}
+        late_gates = []
+        slot_words = {}
+        slot_scales = {}
 
         def load_w1(e):
             rows = w1[e].rearrange("(p j) i -> p j i", j=PACK)
-            raw = w1_pool.tile([P, PACK * H], F32, name="w1_raw")
-            w1_rows[e] = []
-            for lo, hi in zip(W1_LOADS[e], W1_LOADS[e][1:]):
-                piece = raw[:, PACK * PACK * lo : PACK * PACK * hi].rearrange("p (j i) -> p j i", j=PACK)
-                nc.sync.dma_start(piece, rows[:, :, PACK * lo : PACK * hi])
-                w1_rows[e].append((lo, hi, piece.rearrange("p j (m t) -> p m j t", t=PACK)))
+            raw = w1_pool.tile([P, PACK * H + 384], F32, name="w1_raw")
+            bounds = LAST_W1_LOAD if e == LAST else W1_LOAD
+            w1_pieces[e] = []
+            for first, end in zip(bounds, bounds[1:]):
+                piece = raw[:, PACK * PACK * first : PACK * PACK * end].rearrange("p (j i) -> p j i", j=PACK)
+                nc.sync.dma_start(piece, rows[:, :, PACK * first : PACK * end])
+                w1_pieces[e].append((first, end, piece.rearrange("p j (m t) -> p m j t", t=PACK)))
+
+            if e == 10:
+                late_gates.append(raw[:, PACK * H :])
+                nc.sync.dma_start(late_gates[0], gate[:, 1152:])
 
         def load_w2(e, raw):
-            nc.sync.dma_start(raw.rearrange("p a j n -> p a (j n)"), w2[e].rearrange("(a p j) n -> p a (j n)", a=PASSES, j=PACK))
+            nc.sync.dma_start(
+                raw.rearrange("p a j n -> p a (j n)"),
+                w2[e].rearrange("(a p j) n -> p a (j n)", a=PASSES, j=PACK),
+            )
             w2_rows[e] = raw
 
         def load(e):
             load_w1(e)
-            if e < E - 2:
+            if e < 8:
+                if e % 2 == 0:
+                    raw = w2_pool.tile([P, 2, PASSES, PACK, N], F32, name="w2_raw")
+                    nc.sync.dma_start(raw[:].rearrange("p e a j n -> p (e a) (j n)"), w2[e : e + 2].rearrange("e (a p j) n -> p (e a) (j n)", a=PASSES, j=PACK))
+                    w2_rows[e] = raw[:, 0]
+                    w2_rows[e + 1] = raw[:, 1]
+            elif e < LAST - 1:
                 raw = w2_pool.tile([P, PASSES, PACK, N], F32, name="w2_raw")
                 load_w2(e, raw[:])
-            elif e == E - 1:
+            elif e == LAST:
                 raw = w1_pool.tile([P, 2, PASSES, PACK, N], F32, name="w1_raw")
-                load_w2(E - 2, raw[:, 0])
-                load_w2(E - 1, raw[:, 1])
+                load_w2(LAST - 1, raw[:, 0])
+                load_w2(LAST, raw[:, 1])
 
-        def copy_on(engine, dst, src):
-            if engine == "scalar":
-                nc.scalar.copy(dst, src)
-            else:
-                nc.vector.tensor_copy(dst, src)
-
-        def quantize(values, name):
-            width = values.shape[1] // PACK
-            codes = work.tile([P, width], U32, name=name + "_codes", align_bytes=64)
-            scales = work.tile([P, width], U8, name=name + "_scales", align_bytes=64)
-            nc.vector.quantize_mx(codes[:].bitcast(FP8X4), scales[:], values)
-            return codes, scales
-
-        load(0)
-        nc.sync.dma_start(gates[:], gate)
-        load(1)
-        load(2)
-
-        slot_words = {}
-        slot_scales = {}
+        def slot_offsets(first, end):
+            return offsets[:, first // OFFSETS_PER_COLUMN : end // OFFSETS_PER_COLUMN]
 
         def gather(g):
-            piece = offsets[:, g * GATHER // LANES : (g + 1) * GATHER // LANES]
+            picked = slot_offsets(g * GATHER, (g + 1) * GATHER)
             slot_words[g] = keep.tile([P, GATHER], U32, name="slot_words%d" % g, align_bytes=64)
-            nc.vector.tensor_copy(slot_words[g][:], token_words[:].bitcast(U32).indirect(piece))
+            nc.vector.tensor_copy(slot_words[g][:], token_words[:].bitcast(U32).indirect(picked))
             slot_scales[g] = keep.tile([P, GATHER], U8, name="slot_scales%d" % g, align_bytes=64)
-            nc.vector.tensor_copy(slot_scales[g][:], token_scales[:].bitcast(U8).indirect(piece))
+            nc.vector.tensor_copy(slot_scales[g][:], token_scales[:].bitcast(U8).indirect(picked))
 
-        def quantize_blocks(values, name):
-            codes, scales = quantize(values.rearrange("p b c j -> p (b c j)"), name)
-            return [(codes[:, b * P : (b + 1) * P], scales[:, b * P : (b + 1) * P]) for b in range(values.shape[1])]
+        def round_w1(e, a, panels):
+            dst = panels.rearrange("p t m j -> p m j t")
+            for first, end, engine in LAST_W1_COPIES if e == LAST else W1_COPIES:
+                if first // P == a:
+                    origin, src = [(lo, view) for lo, hi, view in w1_pieces[e] if lo <= first and end <= hi][0]
+                    copy[engine](dst[:, first - a * P : end - a * P], src[:, first - origin : end - origin])
 
-        def cast_w1(e, a, blocks):
-            dst = blocks.rearrange("p t m j -> p m j t")
-            for lo, hi, engine in W1_CASTS[e]:
-                if lo // P == a:
-                    first, src = [(start, piece) for start, stop, piece in w1_rows[e] if start <= lo and hi <= stop][0]
-                    copy_on(engine, dst[:, lo - a * P : hi - a * P], src[:, lo - first : hi - first])
-
-        def cast_w2(e, blocks, engines):
+        def round_w2(e, panels, engines):
             for a in range(PASSES):
-                copy_on(
-                    engines[a],
-                    blocks[:, a].rearrange("p (c i) j -> p c j i", i=4),
-                    w2_rows[e][:, a].rearrange("p j (c i) -> p c j i", i=4),
+                copy[engines[a]](
+                    panels[:, a].rearrange("p (c i) j -> p c j i", i=LINE),
+                    w2_rows[e][:, a].rearrange("p j (c i) -> p c j i", i=LINE),
                 )
+
+        def quantize(panels, ring):
+            count = panels.shape[1]
+            codes = work.tile([P, count * P], U32, name=ring + "_codes", align_bytes=64)
+            scales = work.tile([P, count * P], U8, name=ring + "_scales", align_bytes=64)
+            nc.vector.quantize_mx(codes[:].bitcast(FP8X4), scales[:], panels.rearrange("p b c j -> p (b c j)"))
+            return [(codes[:, b * P : (b + 1) * P], scales[:, b * P : (b + 1) * P]) for b in range(count)]
 
         def matmul(dst, stationary, moving, start, stop):
             nc.tensor.matmul_mx(
@@ -145,60 +156,67 @@ def tile_moe_pkd_mlp_relu_kernel(tc, x_words, x_scales, w1, w2, gate, offs, out)
                 stop=stop,
             )
 
-        def first_layer(e, w1_blocks, hidden, engine):
+        def first_layer(e, w1_operands, h_panel):
             g, first = divmod(e * C, GATHER)
             tokens = (slot_words[g][:, first : first + C], slot_scales[g][:, first : first + C])
             bank = a_psum.tile([P, PACK, C], F32, name="a_bank")
             for t in range(PACK):
-                matmul(bank[:, t, :], w1_blocks[t], tokens, True, True)
-            if engine == "scalar":
-                nc.scalar.activation(hidden, bank[:].rearrange("p t s -> p s t"), RELU)
-            else:
-                nc.vector.tensor_scalar_max(hidden, bank[:].rearrange("p t s -> p s t"), 0.0)
+                matmul(bank[:, t, :], w1_operands[t], tokens, True, True)
+            nc.scalar.activation(h_panel, bank[:].rearrange("p t s -> p s t"), RELU)
 
-        def second_layer(e, h_blocks, w2_blocks):
+        def second_layer(e, h_operands, w2_operands):
             bank = y_psum.tile([P, C], F32, name="y_bank")
             for a in range(PASSES):
-                matmul(bank[:], w2_blocks[a], h_blocks[a], a == 0, a == PASSES - 1)
+                matmul(bank[:], w2_operands[a], h_operands[a], a == 0, a == PASSES - 1)
             slots = slice(e * C, (e + 1) * C)
-            nc.vector.tensor_tensor(y_slots[:, slots], bank[:], gates[:, slots], MULT)
-            starts = (0,) + SCATTER_ENDS
-            for start, end in zip(starts, SCATTER_ENDS):
-                if e * C < end <= (e + 1) * C:
-                    piece = offsets[:, start // LANES : end // LANES]
-                    nc.vector.tensor_copy(result[:].indirect(piece), y_slots[:, start:end])
+            nc.vector.tensor_tensor(y_slots[:, slots], bank[:], gates[:, slots] if slots.start < 1152 else late_gates[0][:, slots.start - 1152 : slots.stop - 1152], MULT)
+            for first, end in zip((0,) + SCATTER_ENDS, SCATTER_ENDS):
+                if slots.start < end <= slots.stop:
+                    nc.vector.tensor_copy(result[:].indirect(slot_offsets(first, end)), y_slots[:, first:end])
 
-        batch = work.tile([P, 2 * PACK, P, PACK], BF16, name="batch", align_bytes=64)
-        for e in range(E - 1):
-            if e + 3 < E:
-                load(e + 3)
+        def batch_tile():
+            return work.tile([P, 2 * PACK, P, PACK], BF16, name="batch", align_bytes=64)
+
+        def upper_tile():
+            return work.tile([P, PACK, P, PACK], BF16, name="upper", align_bytes=64)
+
+        load(0)
+        nc.sync.dma_start(gates[:, :1152], gate[:, :1152])
+        for e in range(1, LOAD_AHEAD):
+            load(e)
+
+        batch = batch_tile()
+        for e in range(LAST):
+            if e + LOAD_AHEAD < E:
+                load(e + LOAD_AHEAD)
             if e * C % GATHER == 0:
                 gather(e * C // GATHER)
-            upper = work.tile([P, PACK, P, PACK], BF16, name="upper", align_bytes=64)
-            cast_w1(e, 0, batch[:, :PACK])
-            cast_w1(e, 1, upper[:])
+            upper = upper_tile()
+            round_w1(e, 0, batch[:, W1_PANELS])
+            round_w1(e, 1, upper[:])
             if e > 0:
-                blocks = quantize_blocks(batch[:], "batch")
-                second_layer(e - 1, blocks[PACK : PACK + PASSES], blocks[PACK + PASSES :])
+                operands = quantize(batch[:], "batch")
+                second_layer(e - 1, operands[H_PANELS], operands[W2_PANELS])
             else:
-                blocks = quantize_blocks(batch[:, :PACK], "batch")
-            following = work.tile([P, 2 * PACK, P, PACK], BF16, name="batch", align_bytes=64)
-            first_layer(e, blocks[:PACK], following[:, PACK], "scalar")
-            first_layer(e, quantize_blocks(upper[:], "upper"), following[:, PACK + 1], "scalar")
-            if e < E - 2:
-                cast_w2(e, following[:, PACK + PASSES :], ["scalar", "scalar"])
-            batch = following
-        e = E - 1
-        upper = work.tile([P, PACK, P, PACK], BF16, name="upper", align_bytes=64)
-        following = work.tile([P, 2 * PACK, P, PACK], BF16, name="batch", align_bytes=64)
-        cast_w1(e, 0, batch[:, :PACK])
-        first_layer(e, quantize_blocks(batch[:, :PACK], "batch"), following[:, PACK], "scalar")
-        cast_w2(e - 1, batch[:, PACK + PASSES :], ["scalar","scalar"])
-        blocks = quantize_blocks(batch[:, PACK:], "batch")
-        second_layer(e - 1, blocks[:PASSES], blocks[PASSES:])
-        cast_w1(e, 1, upper[:])
-        first_layer(e, quantize_blocks(upper[:], "upper"), following[:, PACK + 1], "scalar")
-        cast_w2(e, following[:, PACK + PASSES :], ["scalar","vector"])
-        w2_blocks = quantize_blocks(following[:, PACK + PASSES :], "batch")
-        second_layer(e, quantize_blocks(following[:, PACK : PACK + PASSES], "upper"), w2_blocks)
+                operands = quantize(batch[:, W1_PANELS], "batch")
+            next_batch = batch_tile()
+            first_layer(e, operands[W1_PANELS], next_batch[:, H_PANELS.start])
+            first_layer(e, quantize(upper[:], "upper"), next_batch[:, H_PANELS.start + 1])
+            if e < LAST - 1:
+                round_w2(e, next_batch[:, W2_PANELS], ["scalar", "scalar"])
+            batch = next_batch
+
+        upper = upper_tile()
+        next_batch = batch_tile()
+        round_w1(LAST, 0, batch[:, W1_PANELS])
+        first_layer(LAST, quantize(batch[:, W1_PANELS], "batch"), next_batch[:, H_PANELS.start])
+        round_w2(LAST - 1, batch[:, W2_PANELS], ["scalar", "scalar"])
+        operands = quantize(batch[:, SECOND_LAYER_PANELS], "batch")
+        second_layer(LAST - 1, operands[:PASSES], operands[PASSES:])
+        round_w1(LAST, 1, upper[:])
+        first_layer(LAST, quantize(upper[:], "upper"), next_batch[:, H_PANELS.start + 1])
+        round_w2(LAST, next_batch[:, W2_PANELS], ["scalar", "vector"])
+        w2_operands = quantize(next_batch[:, W2_PANELS], "batch")
+        second_layer(LAST, quantize(next_batch[:, H_PANELS], "upper"), w2_operands)
+
         nc.sync.dma_start(out, result[:])

from contextlib import ExitStack

import concourse.mybir as mybir

K, T, E, C, H, N = 512, 1536, 12, 128, 1024, 128
FLOPS = 2 * E * C * (K * H + H * N)

F32 = mybir.dt.float32
BF16 = mybir.dt.bfloat16
I32 = mybir.dt.int32
U32 = mybir.dt.uint32
U16 = mybir.dt.uint16
U8 = mybir.dt.uint8
FP8X4 = mybir.dt.float8_e4m3fn_x4
RELU = mybir.ActivationFunctionType.Relu
MULT = mybir.AluOpType.mult

P = 128
PACK = 4
PASS = P * PACK
PASSES = H // PASS
QUADRANT = 32
OFFSETS_PER_COLUMN = 16
LINE = 4
LAST = E - 1

GATHER = 3 * C
SCATTER_ENDS = (256, 512, 768, 960, 1152, 1344, 1536)

W1_LOAD = (0, 256)
W1_COPIES = ((0, 128, "vector"), (128, 224, "scalar"), (224, 256, "vector"))
LAST_W1_LOAD = (0, 64, 160, 256)
LAST_W1_COPIES = ((0, 64, "scalar"), (64, 128, "vector"), (128, 160, "scalar"), (160, 256, "vector"))

LOAD_AHEAD = 3
STREAM_BUFS = 6
WORK_BUFS = 3
A_BANKS = 4
Y_BANKS = 2

W1_PANELS = slice(0, PACK)
H_PANELS = slice(PACK, PACK + PASSES)
W2_PANELS = slice(PACK + PASSES, 2 * PACK)
SECOND_LAYER_PANELS = slice(PACK, 2 * PACK)


def tile_moe_pkd_mlp_relu_kernel(tc, x_words, x_scales, w1, w2, gate, offs, out):
    nc = tc.nc
    copy = {"scalar": nc.scalar.copy, "vector": nc.vector.tensor_copy}
    with ExitStack() as ctx:
        keep = ctx.enter_context(tc.tile_pool(name="keep", bufs=1))
        w1_pool = ctx.enter_context(tc.tile_pool(name="w1_pool", bufs=STREAM_BUFS))
        w2_pool = ctx.enter_context(tc.tile_pool(name="w2_pool", bufs=4))
        work = ctx.enter_context(tc.tile_pool(name="work", bufs=WORK_BUFS))
        a_psum = ctx.enter_context(tc.psum_pool(name="a_psum", bufs=A_BANKS))
        y_psum = ctx.enter_context(tc.psum_pool(name="y_psum", bufs=Y_BANKS))

        offsets = keep.tile([P, T // OFFSETS_PER_COLUMN], U16)
        nc.sync.dma_start(offsets[:], offs)
        token_words = keep.tile([P, T], I32, align_bytes=64)
        nc.sync.dma_start(token_words[:], x_words[0].rearrange("p t r -> p (t r)").bitcast(I32))
        token_scales = keep.tile([P, T // 4], I32, align_bytes=64)
        nc.vector.memset(token_scales[:], 0)
        for quadrant in range(P // QUADRANT):
            nc.sync.dma_start(
                token_scales[QUADRANT * quadrant : QUADRANT * quadrant + 4, :],
                x_scales[0, 4 * quadrant : 4 * quadrant + 4, :].bitcast(I32),
            )

        gates = keep.tile([P, T], F32)
        y_slots = keep.tile([P, T], F32)
        result = keep.tile([P, T], F32)

        w1_pieces = {}
        w2_rows = {}
        late_gates = []
        slot_words = {}
        slot_scales = {}

        def load_w1(e):
            rows = w1[e].rearrange("(p j) i -> p j i", j=PACK)
            raw = w1_pool.tile([P, PACK * H + 384], F32, name="w1_raw")
            bounds = LAST_W1_LOAD if e == LAST else W1_LOAD
            w1_pieces[e] = []
            for first, end in zip(bounds, bounds[1:]):
                piece = raw[:, PACK * PACK * first : PACK * PACK * end].rearrange("p (j i) -> p j i", j=PACK)
                nc.sync.dma_start(piece, rows[:, :, PACK * first : PACK * end])
                w1_pieces[e].append((first, end, piece.rearrange("p j (m t) -> p m j t", t=PACK)))

            if e == 10:
                late_gates.append(raw[:, PACK * H :])
                nc.sync.dma_start(late_gates[0], gate[:, 1152:])

        def load_w2(e, raw):
            nc.sync.dma_start(
                raw.rearrange("p a j n -> p a (j n)"),
                w2[e].rearrange("(a p j) n -> p a (j n)", a=PASSES, j=PACK),
            )
            w2_rows[e] = raw

        def load(e):
            load_w1(e)
            if e < 8:
                if e % 2 == 0:
                    raw = w2_pool.tile([P, 2, PASSES, PACK, N], F32, name="w2_raw")
                    nc.sync.dma_start(raw[:].rearrange("p e a j n -> p (e a) (j n)"), w2[e : e + 2].rearrange("e (a p j) n -> p (e a) (j n)", a=PASSES, j=PACK))
                    w2_rows[e] = raw[:, 0]
                    w2_rows[e + 1] = raw[:, 1]
            elif e < LAST - 1:
                raw = w2_pool.tile([P, PASSES, PACK, N], F32, name="w2_raw")
                load_w2(e, raw[:])
            elif e == LAST:
                raw = w1_pool.tile([P, 2, PASSES, PACK, N], F32, name="w1_raw")
                load_w2(LAST - 1, raw[:, 0])
                load_w2(LAST, raw[:, 1])

        def slot_offsets(first, end):
            return offsets[:, first // OFFSETS_PER_COLUMN : end // OFFSETS_PER_COLUMN]

        def gather(g):
            picked = slot_offsets(g * GATHER, (g + 1) * GATHER)
            slot_words[g] = keep.tile([P, GATHER], U32, name="slot_words%d" % g, align_bytes=64)
            nc.vector.tensor_copy(slot_words[g][:], token_words[:].bitcast(U32).indirect(picked))
            slot_scales[g] = keep.tile([P, GATHER], U8, name="slot_scales%d" % g, align_bytes=64)
            nc.vector.tensor_copy(slot_scales[g][:], token_scales[:].bitcast(U8).indirect(picked))

        def round_w1(e, a, panels):
            dst = panels.rearrange("p t m j -> p m j t")
            for first, end, engine in LAST_W1_COPIES if e == LAST else W1_COPIES:
                if first // P == a:
                    origin, src = [(lo, view) for lo, hi, view in w1_pieces[e] if lo <= first and end <= hi][0]
                    copy[engine](dst[:, first - a * P : end - a * P], src[:, first - origin : end - origin])

        def round_w2(e, panels, engines):
            for a in range(PASSES):
                copy[engines[a]](
                    panels[:, a].rearrange("p (c i) j -> p c j i", i=LINE),
                    w2_rows[e][:, a].rearrange("p j (c i) -> p c j i", i=LINE),
                )

        def quantize(panels, ring):
            count = panels.shape[1]
            codes = work.tile([P, count * P], U32, name=ring + "_codes", align_bytes=64)
            scales = work.tile([P, count * P], U8, name=ring + "_scales", align_bytes=64)
            nc.vector.quantize_mx(codes[:].bitcast(FP8X4), scales[:], panels.rearrange("p b c j -> p (b c j)"))
            return [(codes[:, b * P : (b + 1) * P], scales[:, b * P : (b + 1) * P]) for b in range(count)]

        def matmul(dst, stationary, moving, start, stop):
            nc.tensor.matmul_mx(
                dst,
                lhsT=stationary[0].bitcast(FP8X4),
                lhsT_scale=stationary[1],
                rhs=moving[0].bitcast(FP8X4),
                rhs_scale=moving[1],
                start=start,
                stop=stop,
            )

        def first_layer(e, w1_operands, h_panel):
            g, first = divmod(e * C, GATHER)
            tokens = (slot_words[g][:, first : first + C], slot_scales[g][:, first : first + C])
            bank = a_psum.tile([P, PACK, C], F32, name="a_bank")
            for t in range(PACK):
                matmul(bank[:, t, :], w1_operands[t], tokens, True, True)
            nc.scalar.activation(h_panel, bank[:].rearrange("p t s -> p s t"), RELU)

        def second_layer(e, h_operands, w2_operands):
            bank = y_psum.tile([P, C], F32, name="y_bank")
            for a in range(PASSES):
                matmul(bank[:], w2_operands[a], h_operands[a], a == 0, a == PASSES - 1)
            slots = slice(e * C, (e + 1) * C)
            nc.vector.tensor_tensor(y_slots[:, slots], bank[:], gates[:, slots] if slots.start < 1152 else late_gates[0][:, slots.start - 1152 : slots.stop - 1152], MULT)
            for first, end in zip((0,) + SCATTER_ENDS, SCATTER_ENDS):
                if slots.start < end <= slots.stop:
                    nc.vector.tensor_copy(result[:].indirect(slot_offsets(first, end)), y_slots[:, first:end])

        def batch_tile():
            return work.tile([P, 2 * PACK, P, PACK], BF16, name="batch", align_bytes=64)

        def upper_tile():
            return work.tile([P, PACK, P, PACK], BF16, name="upper", align_bytes=64)

        load(0)
        nc.sync.dma_start(gates[:, :1152], gate[:, :1152])
        for e in range(1, LOAD_AHEAD):
            load(e)

        batch = batch_tile()
        for e in range(LAST):
            if e + LOAD_AHEAD < E:
                load(e + LOAD_AHEAD)
            if e * C % GATHER == 0:
                gather(e * C // GATHER)
            upper = upper_tile()
            round_w1(e, 0, batch[:, W1_PANELS])
            round_w1(e, 1, upper[:])
            if e > 0:
                operands = quantize(batch[:], "batch")
                second_layer(e - 1, operands[H_PANELS], operands[W2_PANELS])
            else:
                operands = quantize(batch[:, W1_PANELS], "batch")
            next_batch = batch_tile()
            first_layer(e, operands[W1_PANELS], next_batch[:, H_PANELS.start])
            first_layer(e, quantize(upper[:], "upper"), next_batch[:, H_PANELS.start + 1])
            if e < LAST - 1:
                round_w2(e, next_batch[:, W2_PANELS], ["scalar", "scalar"])
            batch = next_batch

        upper = upper_tile()
        next_batch = batch_tile()
        round_w1(LAST, 0, batch[:, W1_PANELS])
        first_layer(LAST, quantize(batch[:, W1_PANELS], "batch"), next_batch[:, H_PANELS.start])
        round_w2(LAST - 1, batch[:, W2_PANELS], ["scalar", "scalar"])
        operands = quantize(batch[:, SECOND_LAYER_PANELS], "batch")
        second_layer(LAST - 1, operands[:PASSES], operands[PASSES:])
        round_w1(LAST, 1, upper[:])
        first_layer(LAST, quantize(upper[:], "upper"), next_batch[:, H_PANELS.start + 1])
        round_w2(LAST, next_batch[:, W2_PANELS], ["scalar", "vector"])
        w2_operands = quantize(next_batch[:, W2_PANELS], "batch")
        second_layer(LAST, quantize(next_batch[:, H_PANELS], "upper"), w2_operands)

        nc.sync.dma_start(out, result[:])
